import numpy as np, ml_dtypes
CORES = [16,17,18,19,150,151]
N = 6
S, B = 4, 256
def setup_inputs(rng):
    a = (rng.standard_normal((128, 128), dtype=np.float32) / 12).astype(ml_dtypes.bfloat16)
    return {"x": rng.standard_normal((N, 128, S * B), dtype=np.float32).astype(ml_dtypes.bfloat16), "a": np.broadcast_to(a, (N, 128, 128)).copy(), "at": np.broadcast_to(a.T, (N, 128, 128)).copy()}
def setup_inputs_big(rng):
    d = setup_inputs(rng)
    for k in ("x",): d[k] = (d[k].astype(np.float32) * 1048576.0).astype(d[k].dtype)
    return d
def setup_inputs_small(rng):
    d = setup_inputs(rng)
    for k in ("x",): d[k] = (d[k].astype(np.float32) * (1 / 1048576.0)).astype(d[k].dtype)
    return d
def setup_inputs_apart(rng):
    d = setup_inputs(rng)
    f = (10.0 ** rng.permutation(np.linspace(-1.5, 1.5, N))).astype(np.float32).reshape(N, 1, 1)
    for k in ("x",): d[k] = (d[k].astype(np.float32) * f).astype(d[k].dtype)
    return d
def reference(x, a, at):
    X, A = x.astype(np.float64), a.astype(np.float64)
    y = np.zeros((N, 128, S * B)); h = np.zeros((128, B))
    for r in range(N):
        for s in range(S):
            h = A[r].T @ h + X[r][:, B * s:B * s + B]
            y[r][:, B * s:B * s + B] = h
    return {"y": y.astype(ml_dtypes.bfloat16)}

@@ -1,0 +1,187 @@
+from concourse.bass import DstId, RemoteDMATransfer
+from concourse.mybir import AluOpType
+
+N, S, B, D = 6, 4, 256, 128
+PW = {1: 0, 2: 1, 3: 2, 4: 3, 8: 4, 12: 5, 16: 6}
+PT = {1: 0, 2: 1, 4: 2, 8: 3}
+
+SCRATCH = {
+    "xs": ("sbuf", [128, S * B], "bfloat16"),
+    "pw": ("sbuf", [128, len(PW) * D], "bfloat16"),
+    "pt": ("sbuf", [128, len(PT) * D], "bfloat16"),
+    "ls": ("sbuf", [128, (S - 1) * B], "bfloat16"),
+    "land": ("sbuf", [128, (N - 1) * B], "bfloat16"),
+    "cb": ("sbuf", [128, B], "bfloat16"),
+    "ys": ("sbuf", [128, S * B], "bfloat16"),
+}
+for i in range(8):
+    SCRATCH["b%d" % i] = ("psum", [128, 512], "float32")
+
+SEMAPHORES = ["lda", "ldt", "ldx0", "ldx1", "pe", "ve", "sent", "st"] + ["arr%d" % q for q in range(N - 1)]
+
+
+def bits_of(m):
+    return [b for b in range(m.bit_length()) if (m >> b) & 1]
+
+
+def trim(m):
+    bits, n = bits_of(m), 1
+    while n * 2 <= len(bits):
+        n *= 2
+    return sum(1 << b for b in bits[:n])
+
+
+def calls_of(q, cores, topo):
+    src = cores[q]
+    here = (topo.host(src), topo.chip(src))
+    later = list(cores[q + 1:])
+    far = [d for d in later if (topo.host(d), topo.chip(d)) != here]
+    near = [d for d in later if (topo.host(d), topo.chip(d)) == here]
+    calls, far_mask = [], 0
+    if far:
+        far_mask = topo.mask(src, far[0])
+        for d in far:
+            far_mask &= topo.mask(src, d)
+        far_mask = trim(far_mask)
+        calls.append((far_mask, far))
+    if near:
+        m = topo.mask(src, near[0])
+        for d in near:
+            m &= topo.mask(src, d)
+        calls.append((trim(m & ~far_mask), near))
+    return calls
+
+
+def rank_program(g, core, T, topo):
+    r = T.rank_of(core)
+    if r is None:
+        return
+    cores = list(T.cores)
+    sem = T.sem
+    queues = {"pe": g.tensor, "ve": g.vector, "sy": g.sync, "sc": g.scalar, "g": g}
+    done = {"pe": 0, "ve": 0}
+    seen = {}
+
+    def need(qn, toks):
+        for name, val in toks:
+            if seen.get((qn, name), 0) < val:
+                queues[qn].wait_ge(sem[name], val)
+                seen[(qn, name)] = val
+
+    def mm(out, lhsT, rhs, deps, start=True, stop=True):
+        need("pe", deps)
+        g.tensor.matmul(out, lhsT, rhs, start, stop).then_inc(sem.pe, 1)
+        done["pe"] += 1
+        return ("pe", done["pe"])
+
+    def vadd(out, in0, in1, deps):
+        need("ve", deps)
+        g.vector.tensor_tensor(out, in0, in1, AluOpType.add).then_inc(sem.ve, 1)
+        done["ve"] += 1
+        return ("ve", done["ve"])
+
+    def vcopy(out, in_, deps):
+        need("ve", deps)
+        g.vector.tensor_copy(out, in_).then_inc(sem.ve, 1)
+        done["ve"] += 1
+        return ("ve", done["ve"])
+
+    def A(k, n=1):
+        return T.pw[:, PW[k] * D:(PW[k] + n) * D]
+
+    def At(k):
+        return T.pt[:, PT[k] * D:(PT[k] + 1) * D]
+
+    def X(s):
+        return T.xs[:, s * B:(s + 1) * B]
+
+    def Lc(s):
+        return X(0) if s == 0 else T.ls[:, (s - 1) * B:s * B]
+
+    def Y(s):
+        return T.ys[:, s * B:(s + 1) * B]
+
+    def land(q):
+        return T.land[:, q * B:(q + 1) * B]
+
+    bank = [T["b%d" % k] for k in range(8)]
+    LA, LT, LX0, LX1 = ("lda", 16), ("ldt", 16), ("ldx0", 16), ("ldx1", 16)
+
+    g.sync.dma_start(A(1), T.a[:]).then_inc(sem.lda, 16)
+    g.scalar.dma_start(T.xs[:, 0:2 * B], T.x[:, 0:2 * B]).then_inc(sem.ldx0, 16)
+    g.sync.dma_start(T.xs[:, 2 * B:4 * B], T.x[:, 2 * B:4 * B]).then_inc(sem.ldx1, 16)
+    if r > 0:
+        g.scalar.dma_start(At(1), T.at[:]).then_inc(sem.ldt, 16)
+
+    tl = [LX0]
+    for s in range(1, S):
+        p = mm(bank[s - 1][:, 0:B], A(1), Lc(s - 1), [LA, tl[s - 1]])
+        tl.append(vadd(Lc(s), bank[s - 1][:, 0:B], X(s), [p, LX0 if s < 2 else LX1]))
+
+    sent = 0
+    if r < N - 1:
+        need("g", [tl[S - 1]])
+        for mask, dsts in calls_of(r, cores, topo):
+            ids = []
+            for d in dsts:
+                rid, pid = topo.addr(d, core)
+                ids.append(DstId(rid=rid, pnc=pid))
+            g.remote_dma_fused(
+                [RemoteDMATransfer(dst_ids=ids, dma_engine_mask=mask, remote_sem=sem["arr%d" % r],
+                                   srcs=[Lc(S - 1)], dsts=[land(r) for d in dsts], alu_op=0)],
+                local_sem=sem.sent)
+            sent += len(bits_of(mask))
+
+    stores = 0
+    if r == 0:
+        need("sy", [LX0])
+        g.sync.dma_start(T.y[:, 0:B], X(0)).then_inc(sem.st, 16)
+        need("sc", [tl[S - 1]])
+        g.scalar.dma_start(T.y[:, B:S * B], T.ls[:]).then_inc(sem.st, 16)
+        stores = 2
+    else:
+        def arrived(q):
+            for mask, dsts in calls_of(q, cores, topo):
+                if core in dsts:
+                    return ("arr%d" % q, len(bits_of(mask)))
+
+        mm(bank[3][:, 0:D], At(1), A(1), [LT, LA])
+        p = mm(bank[3][:, D:2 * D], A(1), At(1), [])
+        vcopy(A(2), bank[3][:, 0:D], [p])
+        t = vcopy(At(2), bank[3][:, D:2 * D], [p])
+        p = mm(bank[4][:, 0:2 * D], At(2), A(1, 2), [t])
+        if r >= 3:
+            p = mm(bank[4][:, 2 * D:3 * D], A(2), At(2), [])
+        t = vcopy(A(3, 2), bank[4][:, 0:2 * D], [p])
+        if r >= 3:
+            t = vcopy(At(4), bank[4][:, 2 * D:3 * D], [p])
+            p = mm(bank[5][:, 0:D], At(4), A(4), [t])
+            if r >= 4:
+                p = mm(bank[5][:, D:2 * D], A(4), At(4), [])
+            t = vcopy(A(8), bank[5][:, 0:D], [p])
+            if r >= 4:
+                t = vcopy(At(8), bank[5][:, D:2 * D], [p])
+                n = r - 3
+                p = mm(bank[6][:, 0:n * D], At(8), A(4, n), [t])
+                t = vcopy(A(12, n), bank[6][:, 0:n * D], [p])
+        tpow = t
+
+        if r == 1:
+            carry, tc = land(0), arrived(0)
+        else:
+            for q in range(r - 1):
+                p = mm(bank[7][:, 0:B], A(4 * (r - 1 - q)), land(q), [tpow, arrived(q)],
+                       start=(q == 0), stop=(q == r - 2))
+            carry = T.cb[:]
+            tc = vadd(carry, bank[7][:, 0:B], land(r - 1), [p, arrived(r - 1)])
+        for s in range(S):
+            p = mm(bank[s][:, 0:B], A(s + 1), carry, [tpow, tc])
+            t = vadd(Y(s), bank[s][:, 0:B], Lc(s), [p, tl[s]])
+            qn = "sy" if s % 2 == 0 else "sc"
+            need(qn, [t])
+            queues[qn].dma_start(T.y[:, s * B:(s + 1) * B], Y(s)).then_inc(sem.st, 16)
+            stores += 1
+
+    if sent:
+        g.wait_ge(sem.sent, sent)
+    g.wait_ge(sem.st, 16 * stores)

@@ -2,6 +2,7 @@ from concourse.bass import DstId, RemoteDMATransfer
 from concourse.mybir import AluOpType
 
 N, S, B, D = 6, 4, 256, 128
+H = B // 2
 PW = {1: 0, 2: 1, 3: 2, 4: 3, 8: 4, 12: 5, 16: 6}
 PT = {1: 0, 2: 1, 4: 2, 8: 3}
 
@@ -37,19 +38,20 @@ def calls_of(q, cores, topo):
     later = list(cores[q + 1:])
     far = [d for d in later if (topo.host(d), topo.chip(d)) != here]
     near = [d for d in later if (topo.host(d), topo.chip(d)) == here]
-    calls, far_mask = [], 0
+    fars, nears, far_mask = [], [], 0
     if far:
         far_mask = topo.mask(src, far[0])
         for d in far:
             far_mask &= topo.mask(src, d)
         far_mask = trim(far_mask)
-        calls.append((far_mask, far))
+        first = (q * len(far)) // cores.index(far[0])
+        fars = [(far_mask, d, turn) for turn, d in enumerate(far[first:] + far[:first])]
     if near:
         m = topo.mask(src, near[0])
         for d in near:
             m &= topo.mask(src, d)
-        calls.append((trim(m & ~far_mask), near))
-    return calls
+        nears = [(trim(m & ~far_mask), d, turn) for turn, d in enumerate(near[::-1])]
+    return fars + nears
 
 
 def rank_program(g, core, T, topo):
@@ -92,17 +94,22 @@ def rank_program(g, core, T, topo):
     def At(k):
         return T.pt[:, PT[k] * D:(PT[k] + 1) * D]
 
-    def X(s):
-        return T.xs[:, s * B:(s + 1) * B]
+    def part(t, blk, h=None):
+        if h is None:
+            return t[:, blk * B:(blk + 1) * B]
+        return t[:, blk * B + h * H:blk * B + (h + 1) * H]
 
-    def Lc(s):
-        return X(0) if s == 0 else T.ls[:, (s - 1) * B:s * B]
+    def X(s, h=None):
+        return part(T.xs, s, h)
 
-    def Y(s):
-        return T.ys[:, s * B:(s + 1) * B]
+    def Lc(s, h=None):
+        return X(0, h) if s == 0 else part(T.ls, s - 1, h)
 
-    def land(q):
-        return T.land[:, q * B:(q + 1) * B]
+    def Y(s, h=None):
+        return part(T.ys, s, h)
+
+    def land(q, h=None):
+        return part(T.land, q, h)
 
     bank = [T["b%d" % k] for k in range(8)]
     LA, LT, LX0, LX1 = ("lda", 16), ("ldt", 16), ("ldx0", 16), ("ldx1", 16)
@@ -113,70 +120,78 @@ def rank_program(g, core, T, topo):
     if r > 0:
         g.scalar.dma_start(At(1), T.at[:]).then_inc(sem.ldt, 16)
 
-    tl = [LX0]
+    tl = [[LX0, LX0]]
     for s in range(1, S):
-        p = mm(bank[s - 1][:, 0:B], A(1), Lc(s - 1), [LA, tl[s - 1]])
-        tl.append(vadd(Lc(s), bank[s - 1][:, 0:B], X(s), [p, LX0 if s < 2 else LX1]))
+        ps = [mm(bank[2 * (s - 1) + h][:, 0:H], A(1), Lc(s - 1, h), [LA, tl[s - 1][h]]) for h in range(2)]
+        tl.append([vadd(Lc(s, h), bank[2 * (s - 1) + h][:, 0:H], X(s, h), [ps[h], LX0 if s < 2 else LX1])
+                   for h in range(2)])
 
     sent = 0
     if r < N - 1:
-        need("g", [tl[S - 1]])
-        for mask, dsts in calls_of(r, cores, topo):
-            ids = []
-            for d in dsts:
-                rid, pid = topo.addr(d, core)
-                ids.append(DstId(rid=rid, pnc=pid))
-            g.remote_dma_fused(
-                [RemoteDMATransfer(dst_ids=ids, dma_engine_mask=mask, remote_sem=sem["arr%d" % r],
-                                   srcs=[Lc(S - 1)], dsts=[land(r) for d in dsts], alu_op=0)],
-                local_sem=sem.sent)
+        need("g", [tl[S - 1][1]])
+        for mask, d, turn in calls_of(r, cores, topo):
+            rid, pid = topo.addr(d, core)
+            g.remote_dma(land(r), Lc(S - 1), sem["arr%d" % r], sem.sent, pid, rid, mask)
             sent += len(bits_of(mask))
 
     stores = 0
     if r == 0:
-        need("sy", [LX0])
+        need("sy", [LX0, ("sent", sent)])
         g.sync.dma_start(T.y[:, 0:B], X(0)).then_inc(sem.st, 16)
-        need("sc", [tl[S - 1]])
+        need("sc", [tl[S - 1][1], ("sent", sent)])
         g.scalar.dma_start(T.y[:, B:S * B], T.ls[:]).then_inc(sem.st, 16)
         stores = 2
     else:
-        def arrived(q):
-            for mask, dsts in calls_of(q, cores, topo):
-                if core in dsts:
-                    return ("arr%d" % q, len(bits_of(mask)))
+        def my_call(q):
+            return [c for c in calls_of(q, cores, topo) if c[1] == core][0]
 
-        mm(bank[3][:, 0:D], At(1), A(1), [LT, LA])
-        p = mm(bank[3][:, D:2 * D], A(1), At(1), [])
-        vcopy(A(2), bank[3][:, 0:D], [p])
-        t = vcopy(At(2), bank[3][:, D:2 * D], [p])
-        p = mm(bank[4][:, 0:2 * D], At(2), A(1, 2), [t])
+        def arrived(q):
+            return ("arr%d" % q, len(bits_of(my_call(q)[0])))
+
+        mm(bank[6][:, 0:D], At(1), A(1), [LT, LA])
+        p = mm(bank[6][:, D:2 * D], A(1), At(1), [])
+        vcopy(A(2), bank[6][:, 0:D], [p, tl[S - 1][1]])
+        t = vcopy(At(2), bank[6][:, D:2 * D], [p])
+        p = mm(bank[7][:, 0:2 * D], At(2), A(1, 2), [t])
         if r >= 3:
-            p = mm(bank[4][:, 2 * D:3 * D], A(2), At(2), [])
-        t = vcopy(A(3, 2), bank[4][:, 0:2 * D], [p])
+            p = mm(bank[7][:, 2 * D:3 * D], A(2), At(2), [])
+        t = vcopy(A(3, 2), bank[7][:, 0:2 * D], [p])
         if r >= 3:
-            t = vcopy(At(4), bank[4][:, 2 * D:3 * D], [p])
-            p = mm(bank[5][:, 0:D], At(4), A(4), [t])
+            t = vcopy(At(4), bank[7][:, 2 * D:3 * D], [p])
+            p = mm(bank[0][:, 0:D], At(4), A(4), [t])
             if r >= 4:
-                p = mm(bank[5][:, D:2 * D], A(4), At(4), [])
-            t = vcopy(A(8), bank[5][:, 0:D], [p])
+                p = mm(bank[0][:, D:2 * D], A(4), At(4), [])
+            t = vcopy(A(8), bank[0][:, 0:D], [p])
             if r >= 4:
-                t = vcopy(At(8), bank[5][:, D:2 * D], [p])
+                t = vcopy(At(8), bank[0][:, D:2 * D], [p])
                 n = r - 3
-                p = mm(bank[6][:, 0:n * D], At(8), A(4, n), [t])
-                t = vcopy(A(12, n), bank[6][:, 0:n * D], [p])
+                p = mm(bank[1][:, 0:n * D], At(8), A(4, n), [t])
+                t = vcopy(A(12, n), bank[1][:, 0:n * D], [p])
         tpow = t
 
         if r == 1:
-            carry, tc = land(0), arrived(0)
+            carry, tc = T.land, [arrived(0), arrived(0)]
         else:
-            for q in range(r - 1):
-                p = mm(bank[7][:, 0:B], A(4 * (r - 1 - q)), land(q), [tpow, arrived(q)],
-                       start=(q == 0), stop=(q == r - 2))
-            carry = T.cb[:]
-            tc = vadd(carry, bank[7][:, 0:B], land(r - 1), [p, arrived(r - 1)])
+            qs = sorted(range(r - 1), key=lambda q: my_call(q)[2])
+            last = my_call(qs[-1])[2]
+            early = [q for q in qs if my_call(q)[2] < last]
+            late = [q for q in qs if my_call(q)[2] == last]
+            seq = [(q, h) for q in early for h in range(2)] + [(q, h) for h in range(2) for q in late]
+            ps = [None, None]
+            for q, h in seq:
+                ps[h] = mm(bank[2 + h][:, 0:H], A(4 * (r - 1 - q)), land(q, h), [tpow, arrived(q)],
+                           start=(q == qs[0]), stop=(q == qs[-1]))
+            carry = T.cb
+            tc = [vadd(part(carry, 0, h), bank[2 + h][:, 0:H], land(r - 1, h), [arrived(r - 1), ps[h]])
+                  for h in range(2)]
         for s in range(S):
-            p = mm(bank[s][:, 0:B], A(s + 1), carry, [tpow, tc])
-            t = vadd(Y(s), bank[s][:, 0:B], Lc(s), [p, tl[s]])
+            if s == 0:
+                ps = [mm(bank[4 + h][:, 0:H], A(1), part(carry, 0, h), [tpow, tc[h]]) for h in range(2)]
+                for h in range(2):
+                    t = vadd(Y(0, h), bank[4 + h][:, 0:H], Lc(0, h), [ps[h], tl[0][h]])
+            else:
+                p = mm(bank[(5 + s) % 8][:, 0:B], A(s + 1), part(carry, 0), [tpow, tc[1]])
+                t = vadd(Y(s), bank[(5 + s) % 8][:, 0:B], Lc(s), [p, tl[s][1]])
             qn = "sy" if s % 2 == 0 else "sc"
             need(qn, [t])
             queues[qn].dma_start(T.y[:, s * B:(s + 1) * B], Y(s)).then_inc(sem.st, 16)

@@ -2,8 +2,8 @@ from concourse.bass import DstId, RemoteDMATransfer
 from concourse.mybir import AluOpType
 
 N, S, B, D = 6, 4, 256, 128
-H = B // 2
-PW = {1: 0, 2: 1, 3: 2, 4: 3, 8: 4, 12: 5, 16: 6}
+HW = B // 2
+PW = {1: 0, 2: 1, 3: 2, 4: 3, 5: 4, 6: 5, 7: 6, 8: 7, 12: 8}
 PT = {1: 0, 2: 1, 4: 2, 8: 3}
 
 SCRATCH = {
@@ -12,13 +12,16 @@ SCRATCH = {
     "pt": ("sbuf", [128, len(PT) * D], "bfloat16"),
     "ls": ("sbuf", [128, (S - 1) * B], "bfloat16"),
     "land": ("sbuf", [128, (N - 1) * B], "bfloat16"),
+    "hs": ("sbuf", [128, B], "bfloat16"),
+    "hl": ("sbuf", [128, B], "bfloat16"),
     "cb": ("sbuf", [128, B], "bfloat16"),
+    "bs": ("sbuf", [128, S * B], "bfloat16"),
     "ys": ("sbuf", [128, S * B], "bfloat16"),
 }
 for i in range(8):
     SCRATCH["b%d" % i] = ("psum", [128, 512], "float32")
 
-SEMAPHORES = ["lda", "ldt", "ldx0", "ldx1", "pe", "ve", "sent", "st"] + ["arr%d" % q for q in range(N - 1)]
+SEMAPHORES = ["lda", "ldt", "ldx0", "ldx1", "pe", "ve", "sent", "st", "arrh"] + ["arr%d" % q for q in range(N - 1)]
 
 
 def bits_of(m):
@@ -32,26 +35,34 @@ def trim(m):
     return sum(1 << b for b in bits[:n])
 
 
-def calls_of(q, cores, topo):
-    src = cores[q]
-    here = (topo.host(src), topo.chip(src))
-    later = list(cores[q + 1:])
-    far = [d for d in later if (topo.host(d), topo.chip(d)) != here]
-    near = [d for d in later if (topo.host(d), topo.chip(d)) == here]
-    fars, nears, far_mask = [], [], 0
-    if far:
-        far_mask = topo.mask(src, far[0])
-        for d in far:
-            far_mask &= topo.mask(src, d)
-        far_mask = trim(far_mask)
-        first = (q * len(far)) // cores.index(far[0])
-        fars = [(far_mask, d, turn) for turn, d in enumerate(far[first:] + far[:first])]
-    if near:
-        m = topo.mask(src, near[0])
-        for d in near:
-            m &= topo.mask(src, d)
-        nears = [(trim(m & ~far_mask), d, turn) for turn, d in enumerate(near[::-1])]
-    return fars + nears
+def groups(cores, topo):
+    place = [(topo.host(c), topo.chip(c)) for c in cores]
+    first = [i for i in range(len(cores)) if place[i] == place[0]]
+    rest = [i for i in range(len(cores)) if place[i] != place[0]]
+    feeds = {first[-1 - j]: d for j, d in enumerate(rest)}
+    return first, rest, feeds
+
+
+def plan(q, cores, topo):
+    first, rest, feeds = groups(cores, topo)
+    mine = first if q in first else rest
+    urgent = [d for d in mine[::-1] if d != q and d in feeds]
+    calm = [d for d in mine[::-1] if d > q and d not in feeds]
+    src, m = cores[q], None
+    for d in urgent + calm + ([feeds[q]] if q in feeds else []):
+        md = topo.mask(src, cores[d])
+        m = md if m is None else m & md
+    if m is None:
+        return [], 0
+    bits, calls = bits_of(m), []
+    if urgent:
+        per = 1
+        while per * 2 * len(urgent) <= len(bits):
+            per *= 2
+        calls.append([(sum(1 << b for b in bits[i * per:(i + 1) * per]), d) for i, d in enumerate(urgent)])
+    for d in calm:
+        calls.append([(trim(m), d)])
+    return calls, trim(m)
 
 
 def rank_program(g, core, T, topo):
@@ -60,9 +71,19 @@ def rank_program(g, core, T, topo):
         return
     cores = list(T.cores)
     sem = T.sem
+    first, rest, feeds = groups(cores, topo)
+    K = len(first)
     queues = {"pe": g.tensor, "ve": g.vector, "sy": g.sync, "sc": g.scalar, "g": g}
     done = {"pe": 0, "ve": 0}
     seen = {}
+    bank = [T["b%d" % k] for k in range(8)]
+    last_on = {}
+    nxt = [6]
+
+    def nb():
+        b = nxt[0]
+        nxt[0] = (b + 1) % 8
+        return b
 
     def need(qn, toks):
         for name, val in toks:
@@ -70,22 +91,25 @@ def rank_program(g, core, T, topo):
                 queues[qn].wait_ge(sem[name], val)
                 seen[(qn, name)] = val
 
-    def mm(out, lhsT, rhs, deps, start=True, stop=True):
-        need("pe", deps)
-        g.tensor.matmul(out, lhsT, rhs, start, stop).then_inc(sem.pe, 1)
+    def mm(b, lo, hi, lhsT, rhs, deps, start=True, stop=True):
+        need("pe", list(deps) + last_on.get((b, "ve"), []))
+        g.tensor.matmul(bank[b][:, lo:hi], lhsT, rhs, start, stop).then_inc(sem.pe, 1)
         done["pe"] += 1
+        last_on[(b, "pe")] = [("pe", done["pe"])]
         return ("pe", done["pe"])
 
-    def vadd(out, in0, in1, deps):
-        need("ve", deps)
-        g.vector.tensor_tensor(out, in0, in1, AluOpType.add).then_inc(sem.ve, 1)
+    def vadd(out, b, lo, hi, in1, deps):
+        need("ve", list(deps) + last_on[(b, "pe")])
+        g.vector.tensor_tensor(out, bank[b][:, lo:hi], in1, AluOpType.add).then_inc(sem.ve, 1)
         done["ve"] += 1
+        last_on[(b, "ve")] = [("ve", done["ve"])]
         return ("ve", done["ve"])
 
-    def vcopy(out, in_, deps):
-        need("ve", deps)
-        g.vector.tensor_copy(out, in_).then_inc(sem.ve, 1)
+    def vcopy(out, b, lo, hi):
+        need("ve", last_on[(b, "pe")])
+        g.vector.tensor_copy(out, bank[b][:, lo:hi]).then_inc(sem.ve, 1)
         done["ve"] += 1
+        last_on[(b, "ve")] = [("ve", done["ve"])]
         return ("ve", done["ve"])
 
     def A(k, n=1):
@@ -97,7 +121,7 @@ def rank_program(g, core, T, topo):
     def part(t, blk, h=None):
         if h is None:
             return t[:, blk * B:(blk + 1) * B]
-        return t[:, blk * B + h * H:blk * B + (h + 1) * H]
+        return t[:, blk * B + h * HW:blk * B + (h + 1) * HW]
 
     def X(s, h=None):
         return part(T.xs, s, h)
@@ -111,7 +135,6 @@ def rank_program(g, core, T, topo):
     def land(q, h=None):
         return part(T.land, q, h)
 
-    bank = [T["b%d" % k] for k in range(8)]
     LA, LT, LX0, LX1 = ("lda", 16), ("ldt", 16), ("ldx0", 16), ("ldx1", 16)
 
     g.sync.dma_start(A(1), T.a[:]).then_inc(sem.lda, 16)
@@ -122,81 +145,143 @@ def rank_program(g, core, T, topo):
 
     tl = [[LX0, LX0]]
     for s in range(1, S):
-        ps = [mm(bank[2 * (s - 1) + h][:, 0:H], A(1), Lc(s - 1, h), [LA, tl[s - 1][h]]) for h in range(2)]
-        tl.append([vadd(Lc(s, h), bank[2 * (s - 1) + h][:, 0:H], X(s, h), [ps[h], LX0 if s < 2 else LX1])
-                   for h in range(2)])
+        for h in range(2):
+            mm(2 * (s - 1) + h, 0, HW, A(1), Lc(s - 1, h), [LA, tl[s - 1][h]])
+        tl.append([vadd(Lc(s, h), 2 * (s - 1) + h, 0, HW, X(s, h), [LX0 if s < 2 else LX1]) for h in range(2)])
 
+    calls, my_mask = plan(r, cores, topo)
     sent = 0
-    if r < N - 1:
+    if calls:
         need("g", [tl[S - 1][1]])
-        for mask, d, turn in calls_of(r, cores, topo):
-            rid, pid = topo.addr(d, core)
+    for call in calls:
+        if len(call) == 1:
+            mask, d = call[0]
+            rid, pid = topo.addr(cores[d], core)
             g.remote_dma(land(r), Lc(S - 1), sem["arr%d" % r], sem.sent, pid, rid, mask)
-            sent += len(bits_of(mask))
-
-    stores = 0
-    if r == 0:
-        need("sy", [LX0, ("sent", sent)])
-        g.sync.dma_start(T.y[:, 0:B], X(0)).then_inc(sem.st, 16)
-        need("sc", [tl[S - 1][1], ("sent", sent)])
-        g.scalar.dma_start(T.y[:, B:S * B], T.ls[:]).then_inc(sem.st, 16)
-        stores = 2
-    else:
-        def my_call(q):
-            return [c for c in calls_of(q, cores, topo) if c[1] == core][0]
-
-        def arrived(q):
-            return ("arr%d" % q, len(bits_of(my_call(q)[0])))
-
-        mm(bank[6][:, 0:D], At(1), A(1), [LT, LA])
-        p = mm(bank[6][:, D:2 * D], A(1), At(1), [])
-        vcopy(A(2), bank[6][:, 0:D], [p, tl[S - 1][1]])
-        t = vcopy(At(2), bank[6][:, D:2 * D], [p])
-        p = mm(bank[7][:, 0:2 * D], At(2), A(1, 2), [t])
-        if r >= 3:
-            p = mm(bank[7][:, 2 * D:3 * D], A(2), At(2), [])
-        t = vcopy(A(3, 2), bank[7][:, 0:2 * D], [p])
-        if r >= 3:
-            t = vcopy(At(4), bank[7][:, 2 * D:3 * D], [p])
-            p = mm(bank[0][:, 0:D], At(4), A(4), [t])
-            if r >= 4:
-                p = mm(bank[0][:, D:2 * D], A(4), At(4), [])
-            t = vcopy(A(8), bank[0][:, 0:D], [p])
-            if r >= 4:
-                t = vcopy(At(8), bank[0][:, D:2 * D], [p])
-                n = r - 3
-                p = mm(bank[1][:, 0:n * D], At(8), A(4, n), [t])
-                t = vcopy(A(12, n), bank[1][:, 0:n * D], [p])
-        tpow = t
-
-        if r == 1:
-            carry, tc = T.land, [arrived(0), arrived(0)]
         else:
-            qs = sorted(range(r - 1), key=lambda q: my_call(q)[2])
-            last = my_call(qs[-1])[2]
-            early = [q for q in qs if my_call(q)[2] < last]
-            late = [q for q in qs if my_call(q)[2] == last]
-            seq = [(q, h) for q in early for h in range(2)] + [(q, h) for h in range(2) for q in late]
-            ps = [None, None]
-            for q, h in seq:
-                ps[h] = mm(bank[2 + h][:, 0:H], A(4 * (r - 1 - q)), land(q, h), [tpow, arrived(q)],
-                           start=(q == qs[0]), stop=(q == qs[-1]))
-            carry = T.cb
-            tc = [vadd(part(carry, 0, h), bank[2 + h][:, 0:H], land(r - 1, h), [arrived(r - 1), ps[h]])
-                  for h in range(2)]
-        for s in range(S):
+            trs = []
+            for mask, d in call:
+                rid, pid = topo.addr(cores[d], core)
+                trs.append(RemoteDMATransfer(dst_ids=[DstId(rid=rid, pnc=pid)], dma_engine_mask=mask,
+                                             remote_sem=sem["arr%d" % r], src=Lc(S - 1), dst=land(r)))
+            g.remote_dma_fused(trs, local_sem=sem.sent)
+        sent += sum(len(bits_of(mask)) for mask, d in call)
+    if r in feeds:
+        sent += len(bits_of(my_mask))
+
+    def arrived(q):
+        n = [len(bits_of(mask)) for call in plan(q, cores, topo)[0] for mask, d in call if d == r][0]
+        return ("arr%d" % q, n)
+
+    stores = [0]
+
+    def store(s, src, deps):
+        qn = "sy" if s % 2 == 0 else "sc"
+        need(qn, deps)
+        queues[qn].dma_start(T.y[:, s * B:(s + 1) * B], src).then_inc(sem.st, 16)
+        stores[0] += 1
+
+    behind = [("sent", sent)] if (r in feeds or r == 0) else []
+
+    tA, tT = {1: LA}, {1: LT}
+
+    def emit_y(carry, tc, koff, base, tbase, count):
+        for s in range(count):
+            k = koff + s + 1
             if s == 0:
-                ps = [mm(bank[4 + h][:, 0:H], A(1), part(carry, 0, h), [tpow, tc[h]]) for h in range(2)]
+                bb = [nb(), nb()]
                 for h in range(2):
-                    t = vadd(Y(0, h), bank[4 + h][:, 0:H], Lc(0, h), [ps[h], tl[0][h]])
+                    mm(bb[h], 0, HW, A(k), carry(h), [tA[k], tc[h]])
+                for h in range(2):
+                    t = vadd(Y(0, h), bb[h], 0, HW, base(0, h), [tbase[0]])
             else:
-                p = mm(bank[(5 + s) % 8][:, 0:B], A(s + 1), part(carry, 0), [tpow, tc[1]])
-                t = vadd(Y(s), bank[(5 + s) % 8][:, 0:B], Lc(s), [p, tl[s][1]])
-            qn = "sy" if s % 2 == 0 else "sc"
-            need(qn, [t])
-            queues[qn].dma_start(T.y[:, s * B:(s + 1) * B], Y(s)).then_inc(sem.st, 16)
-            stores += 1
+                b = nb()
+                mm(b, 0, B, A(k), carry(None), [tA[k], tc[0], tc[1]])
+                t = vadd(Y(s), b, 0, B, base(s, None), [tbase[s]])
+            store(s, Y(s), [t] + behind)
+
+    tls = [tl[s][1] for s in range(S)]
+
+    if r == 0:
+        need("sy", [LX0] + behind)
+        g.sync.dma_start(T.y[:, 0:B], X(0)).then_inc(sem.st, 16)
+        need("sc", [tl[S - 1][1]] + behind)
+        g.scalar.dma_start(T.y[:, B:S * B], T.ls[:]).then_inc(sem.st, 16)
+        stores[0] = 2
+    else:
+        deep = r in feeds or r in rest[1:]
+        b = nb()
+        mm(b, 0, D, At(1), A(1), [LT, LA])
+        mm(b, D, 2 * D, A(1), At(1), [])
+        tA[2] = vcopy(A(2), b, 0, D)
+        tT[2] = vcopy(At(2), b, D, 2 * D)
+        b = nb()
+        mm(b, 0, 2 * D, At(2), A(1, 2), [tA[2], tT[2]])
+        if deep:
+            mm(b, 2 * D, 3 * D, A(2), At(2), [])
+        tA[3] = tA[4] = vcopy(A(3, 2), b, 0, 2 * D)
+        if deep:
+            tT[4] = vcopy(At(4), b, 2 * D, 3 * D)
+        if r in feeds:
+            b = nb()
+            mm(b, 0, D, At(4), A(4), [tA[4], tT[4]])
+            mm(b, D, 2 * D, A(4), At(4), [])
+            tA[8] = vcopy(A(8), b, 0, D)
+            tT[8] = vcopy(At(8), b, D, 2 * D)
+            b = nb()
+            mm(b, 0, D, At(8), A(4), [tT[8]])
+            tA[12] = vcopy(A(12), b, 0, D)
+        elif deep:
+            b = nb()
+            mm(b, 0, 4 * D, At(4), A(1, 4), [tA[4], tT[4]])
+            tA[5] = tA[6] = tA[7] = tA[8] = vcopy(A(5, 4), b, 0, 4 * D)
+
+        if r in feeds:
+            def Lq(q, h):
+                return Lc(S - 1, h) if q == r else land(q, h)
+
+            def tq(q, h):
+                return tl[S - 1][h] if q == r else arrived(q)
+
+            qs = ([r] if r != K - 1 else []) + [q for q in range(K - 2, -1, -1) if q != r]
+            hb = [nb(), nb()]
+            for q in qs:
+                for h in range(2):
+                    k = 4 * (K - 1 - q)
+                    mm(hb[h], 0, HW, A(k), Lq(q, h), [tA[k], tq(q, h)], start=(q == qs[0]), stop=(q == qs[-1]))
+            th = [vadd(part(T.hs, 0, h), hb[h], 0, HW, Lq(K - 1, h), [tq(K - 1, h)]) for h in range(2)]
+            need("g", [th[1]])
+            rid, pid = topo.addr(cores[feeds[r]], core)
+            g.remote_dma(T.hl[:], T.hs[:], sem.arrh, sem.sent, pid, rid, my_mask)
+
+        if r in first:
+            if r == 1:
+                emit_y(lambda h: land(0, h), [arrived(0), arrived(0)], 0, Lc, tls, S)
+            else:
+                cbk = [nb(), nb()]
+                qs = list(range(r - 1))
+                for q in qs:
+                    for h in range(2):
+                        k = 4 * (r - 1 - q)
+                        mm(cbk[h], 0, HW, A(k), land(q, h), [tA[k], arrived(q)], start=(q == qs[0]), stop=(q == qs[-1]))
+                tc = [vadd(part(T.cb, 0, h), cbk[h], 0, HW, land(r - 1, h), [arrived(r - 1)]) for h in range(2)]
+                whole = S - 1 if r == K - 1 else S
+                emit_y(lambda h: part(T.cb, 0, h), tc, 0, Lc, tls, whole)
+                if whole < S:
+                    store(S - 1, T.hs[:], [th[1]] + behind)
+        else:
+            src_rank = [f for f in feeds if feeds[f] == r][0]
+            th = ("arrh", len(bits_of(plan(src_rank, cores, topo)[1])))
+            if r == rest[0]:
+                emit_y(lambda h: part(T.hl, 0, h), [th, th], 0, Lc, tls, S)
+            else:
+                tb = []
+                for s in range(S):
+                    b = nb()
+                    mm(b, 0, B, A(s + 1), land(r - 1), [tA[s + 1], arrived(r - 1)])
+                    tb.append(vadd(part(T.bs, s), b, 0, B, Lc(s), [tls[s]]))
+                emit_y(lambda h: part(T.hl, 0, h), [th, th], S, lambda s, h: part(T.bs, s, h), tb, S)
 
     if sent:
         g.wait_ge(sem.sent, sent)
-    g.wait_ge(sem.st, 16 * stores)
+    g.wait_ge(sem.st, 16 * stores[0])

@@ -4,7 +4,7 @@ from concourse.mybir import AluOpType
 N, S, B, D = 6, 4, 256, 128
 HW = B // 2
 PW = {1: 0, 2: 1, 3: 2, 4: 3, 5: 4, 6: 5, 7: 6, 8: 7, 12: 8}
-PT = {1: 0, 2: 1, 4: 2, 8: 3}
+PT = {1: 0, 2: 1, 4: 2}
 
 SCRATCH = {
     "xs": ("sbuf", [128, S * B], "bfloat16"),
@@ -21,7 +21,8 @@ SCRATCH = {
 for i in range(8):
     SCRATCH["b%d" % i] = ("psum", [128, 512], "float32")
 
-SEMAPHORES = ["lda", "ldt", "ldx0", "ldx1", "pe", "ve", "sent", "st", "arrh"] + ["arr%d" % q for q in range(N - 1)]
+SEMAPHORES = (["lda", "ldt", "ldx0", "ldx1", "pe", "ve", "sent", "st", "arrh0", "arrh1"]
+              + ["arr%d" % q for q in range(N - 1)])
 
 
 def bits_of(m):
@@ -39,7 +40,7 @@ def groups(cores, topo):
     place = [(topo.host(c), topo.chip(c)) for c in cores]
     first = [i for i in range(len(cores)) if place[i] == place[0]]
     rest = [i for i in range(len(cores)) if place[i] != place[0]]
-    feeds = {first[-1 - j]: d for j, d in enumerate(rest)}
+    feeds = {first[-2 - j]: d for j, d in enumerate(rest)}
     return first, rest, feeds
 
 
@@ -62,7 +63,7 @@ def plan(q, cores, topo):
         calls.append([(sum(1 << b for b in bits[i * per:(i + 1) * per]), d) for i, d in enumerate(urgent)])
     for d in calm:
         calls.append([(trim(m), d)])
-    return calls, trim(m)
+    return calls, (trim(m) if q in feeds else 0)
 
 
 def rank_program(g, core, T, topo):
@@ -79,9 +80,12 @@ def rank_program(g, core, T, topo):
     bank = [T["b%d" % k] for k in range(8)]
     last_on = {}
     nxt = [6]
+    kept = []
 
     def nb():
         b = nxt[0]
+        while b in kept:
+            b = (b + 1) % 8
         nxt[0] = (b + 1) % 8
         return b
 
@@ -149,7 +153,7 @@ def rank_program(g, core, T, topo):
             mm(2 * (s - 1) + h, 0, HW, A(1), Lc(s - 1, h), [LA, tl[s - 1][h]])
         tl.append([vadd(Lc(s, h), 2 * (s - 1) + h, 0, HW, X(s, h), [LX0 if s < 2 else LX1]) for h in range(2)])
 
-    calls, my_mask = plan(r, cores, topo)
+    calls, far_mask = plan(r, cores, topo)
     sent = 0
     if calls:
         need("g", [tl[S - 1][1]])
@@ -166,8 +170,7 @@ def rank_program(g, core, T, topo):
                                              remote_sem=sem["arr%d" % r], src=Lc(S - 1), dst=land(r)))
             g.remote_dma_fused(trs, local_sem=sem.sent)
         sent += sum(len(bits_of(mask)) for mask, d in call)
-    if r in feeds:
-        sent += len(bits_of(my_mask))
+    sent += 2 * len(bits_of(far_mask))
 
     def arrived(q):
         n = [len(bits_of(mask)) for call in plan(q, cores, topo)[0] for mask, d in call if d == r][0]
@@ -175,67 +178,60 @@ def rank_program(g, core, T, topo):
 
     stores = [0]
 
-    def store(s, src, deps):
-        qn = "sy" if s % 2 == 0 else "sc"
+    def store(s, n, deps):
+        qn = "sy" if stores[0] % 2 == 0 else "sc"
         need(qn, deps)
-        queues[qn].dma_start(T.y[:, s * B:(s + 1) * B], src).then_inc(sem.st, 16)
+        queues[qn].dma_start(T.y[:, s * B:(s + n) * B], T.ys[:, s * B:(s + n) * B]).then_inc(sem.st, 16)
         stores[0] += 1
 
-    behind = [("sent", sent)] if (r in feeds or r == 0) else []
+    pairs = r in feeds
 
     tA, tT = {1: LA}, {1: LT}
 
-    def emit_y(carry, tc, koff, base, tbase, count):
-        for s in range(count):
-            k = koff + s + 1
-            if s == 0:
+    def emit_y(carry, tc):
+        for s in range(S):
+            k = s + 1
+            if s in (0, S - 1):
                 bb = [nb(), nb()]
                 for h in range(2):
                     mm(bb[h], 0, HW, A(k), carry(h), [tA[k], tc[h]])
                 for h in range(2):
-                    t = vadd(Y(0, h), bb[h], 0, HW, base(0, h), [tbase[0]])
+                    t = vadd(Y(s, h), bb[h], 0, HW, Lc(s, h), [tls[s]])
             else:
                 b = nb()
                 mm(b, 0, B, A(k), carry(None), [tA[k], tc[0], tc[1]])
-                t = vadd(Y(s), b, 0, B, base(s, None), [tbase[s]])
-            store(s, Y(s), [t] + behind)
+                t = vadd(Y(s), b, 0, B, Lc(s), [tls[s]])
+            if not pairs:
+                store(s, 1, [t])
+            elif s % 2 == 1:
+                store(s - 1, 2, [t])
+
+    def emit_far(koff, base, tbase, th):
+        for h in range(2):
+            for s in range(S):
+                k = koff + s + 1
+                b = nb()
+                mm(b, 0, HW, A(k), part(T.hl, 0, h), [tA[k], th[h]])
+                t = vadd(Y(s, h), b, 0, HW, base(s, h), [tbase[s]])
+                if h == 1:
+                    store(s, 1, [t])
 
     tls = [tl[s][1] for s in range(S)]
 
     if r == 0:
-        need("sy", [LX0] + behind)
+        need("sy", [LX0, ("sent", sent)])
         g.sync.dma_start(T.y[:, 0:B], X(0)).then_inc(sem.st, 16)
-        need("sc", [tl[S - 1][1]] + behind)
+        need("sc", [tl[S - 1][1], ("sent", sent)])
         g.scalar.dma_start(T.y[:, B:S * B], T.ls[:]).then_inc(sem.st, 16)
         stores[0] = 2
     else:
-        deep = r in feeds or r in rest[1:]
-        b = nb()
-        mm(b, 0, D, At(1), A(1), [LT, LA])
-        mm(b, D, 2 * D, A(1), At(1), [])
-        tA[2] = vcopy(A(2), b, 0, D)
-        tT[2] = vcopy(At(2), b, D, 2 * D)
-        b = nb()
-        mm(b, 0, 2 * D, At(2), A(1, 2), [tA[2], tT[2]])
-        if deep:
-            mm(b, 2 * D, 3 * D, A(2), At(2), [])
-        tA[3] = tA[4] = vcopy(A(3, 2), b, 0, 2 * D)
-        if deep:
-            tT[4] = vcopy(At(4), b, 2 * D, 3 * D)
-        if r in feeds:
+        def power(out, lhsT, rhs, n, deps):
             b = nb()
-            mm(b, 0, D, At(4), A(4), [tA[4], tT[4]])
-            mm(b, D, 2 * D, A(4), At(4), [])
-            tA[8] = vcopy(A(8), b, 0, D)
-            tT[8] = vcopy(At(8), b, D, 2 * D)
-            b = nb()
-            mm(b, 0, D, At(8), A(4), [tT[8]])
-            tA[12] = vcopy(A(12), b, 0, D)
-        elif deep:
-            b = nb()
-            mm(b, 0, 4 * D, At(4), A(1, 4), [tA[4], tT[4]])
-            tA[5] = tA[6] = tA[7] = tA[8] = vcopy(A(5, 4), b, 0, 4 * D)
+            mm(b, 0, n * D, lhsT, rhs, deps)
+            return vcopy(out, b, 0, n * D)
 
+        tA[2] = power(A(2), At(1), A(1), 1, [LT, LA])
+        tT[2] = power(At(2), A(1), At(1), 1, [])
         if r in feeds:
             def Lq(q, h):
                 return Lc(S - 1, h) if q == r else land(q, h)
@@ -243,20 +239,39 @@ def rank_program(g, core, T, topo):
             def tq(q, h):
                 return tl[S - 1][h] if q == r else arrived(q)
 
-            qs = ([r] if r != K - 1 else []) + [q for q in range(K - 2, -1, -1) if q != r]
+            qs = sorted(range(K - 1), key=lambda q: (q != r, q not in feeds, -q))
             hb = [nb(), nb()]
+            kept.extend(hb)
+
+            def term(q, h):
+                k = 4 * (K - 1 - q)
+                mm(hb[h], 0, HW, A(k), Lq(q, h), [tA[k], tq(q, h)], start=(q == qs[0]), stop=(q == qs[-1]))
+
+            tA[4] = power(A(4), At(2), A(2), 1, [tA[2], tT[2]])
+            tT[4] = power(At(4), A(2), At(2), 1, [])
+            tA[3] = power(A(3), At(2), A(1), 1, [])
+            tA[8] = power(A(8), At(4), A(4), 1, [tA[4], tT[4]])
+            tA[12] = power(A(12), At(4), A(8), 1, [tA[8]])
             for q in qs:
                 for h in range(2):
-                    k = 4 * (K - 1 - q)
-                    mm(hb[h], 0, HW, A(k), Lq(q, h), [tA[k], tq(q, h)], start=(q == qs[0]), stop=(q == qs[-1]))
-            th = [vadd(part(T.hs, 0, h), hb[h], 0, HW, Lq(K - 1, h), [tq(K - 1, h)]) for h in range(2)]
-            need("g", [th[1]])
+                    term(q, h)
+            th = [vadd(part(T.hs, 0, h), hb[h], 0, HW, land(K - 1, h), [arrived(K - 1)]) for h in range(2)]
+            kept.clear()
             rid, pid = topo.addr(cores[feeds[r]], core)
-            g.remote_dma(T.hl[:], T.hs[:], sem.arrh, sem.sent, pid, rid, my_mask)
+            for h in range(2):
+                need("g", [th[h]])
+                g.remote_dma(part(T.hl, 0, h), part(T.hs, 0, h), sem["arrh%d" % h], sem.sent, pid, rid, far_mask)
+        else:
+            tA[3] = tA[4] = power(A(3, 2), At(2), A(1, 2), 2, [tA[2], tT[2]])
+            tT[4] = power(At(4), A(2), At(2), 1, [])
+            if r in rest[1:]:
+                tA[5] = tA[6] = tA[7] = tA[8] = power(A(5, 4), At(4), A(1, 4), 4, [tA[4], tT[4]])
+            elif r in first:
+                tA[8] = power(A(8), At(4), A(4), 1, [tA[4], tT[4]])
 
         if r in first:
             if r == 1:
-                emit_y(lambda h: land(0, h), [arrived(0), arrived(0)], 0, Lc, tls, S)
+                emit_y(lambda h: land(0, h), [arrived(0), arrived(0)])
             else:
                 cbk = [nb(), nb()]
                 qs = list(range(r - 1))
@@ -265,22 +280,20 @@ def rank_program(g, core, T, topo):
                         k = 4 * (r - 1 - q)
                         mm(cbk[h], 0, HW, A(k), land(q, h), [tA[k], arrived(q)], start=(q == qs[0]), stop=(q == qs[-1]))
                 tc = [vadd(part(T.cb, 0, h), cbk[h], 0, HW, land(r - 1, h), [arrived(r - 1)]) for h in range(2)]
-                whole = S - 1 if r == K - 1 else S
-                emit_y(lambda h: part(T.cb, 0, h), tc, 0, Lc, tls, whole)
-                if whole < S:
-                    store(S - 1, T.hs[:], [th[1]] + behind)
+                emit_y(lambda h: part(T.cb, 0, h), tc)
         else:
             src_rank = [f for f in feeds if feeds[f] == r][0]
-            th = ("arrh", len(bits_of(plan(src_rank, cores, topo)[1])))
+            n = len(bits_of(plan(src_rank, cores, topo)[1]))
+            th = [("arrh0", n), ("arrh1", n)]
             if r == rest[0]:
-                emit_y(lambda h: part(T.hl, 0, h), [th, th], 0, Lc, tls, S)
+                emit_far(0, Lc, tls, th)
             else:
                 tb = []
                 for s in range(S):
                     b = nb()
                     mm(b, 0, B, A(s + 1), land(r - 1), [tA[s + 1], arrived(r - 1)])
                     tb.append(vadd(part(T.bs, s), b, 0, B, Lc(s), [tls[s]]))
-                emit_y(lambda h: part(T.hl, 0, h), [th, th], S, lambda s, h: part(T.bs, s, h), tb, S)
+                emit_far(S, lambda s, h: part(T.bs, s, h), tb, th)
 
     if sent:
         g.wait_ge(sem.sent, sent)

@@ -3,6 +3,8 @@ from concourse.mybir import AluOpType
 
 N, S, B, D = 6, 4, 256, 128
 HW = B // 2
+SW = 64
+CP = [(SW, SW + (B - SW) // 2), (SW + (B - SW) // 2, B)]
 PW = {1: 0, 2: 1, 3: 2, 4: 3, 5: 4, 6: 5, 7: 6, 8: 7, 12: 8}
 PT = {1: 0, 2: 1, 4: 2}
 
@@ -12,6 +14,7 @@ SCRATCH = {
     "pt": ("sbuf", [128, len(PT) * D], "bfloat16"),
     "ls": ("sbuf", [128, (S - 1) * B], "bfloat16"),
     "land": ("sbuf", [128, (N - 1) * B], "bfloat16"),
+    "sl": ("sbuf", [128, N * SW], "bfloat16"),
     "hs": ("sbuf", [128, B], "bfloat16"),
     "hl": ("sbuf", [128, B], "bfloat16"),
     "cb": ("sbuf", [128, B], "bfloat16"),
@@ -21,7 +24,7 @@ SCRATCH = {
 for i in range(8):
     SCRATCH["b%d" % i] = ("psum", [128, 512], "float32")
 
-SEMAPHORES = (["lda", "ldt", "ldx0", "ldx1", "pe", "ve", "sent", "st", "arrh0", "arrh1"]
+SEMAPHORES = (["lda", "ldt", "ldx0", "ldx1", "pe", "ve", "sent", "st", "arrh0", "arrh1", "ars"]
               + ["arr%d" % q for q in range(N - 1)])
 
 
@@ -34,6 +37,13 @@ def trim(m):
     while n * 2 <= len(bits):
         n *= 2
     return sum(1 << b for b in bits[:n])
+
+
+def split(m, ds):
+    bits, per = bits_of(m), 1
+    while per * 2 * len(ds) <= len(bits):
+        per *= 2
+    return [(sum(1 << b for b in bits[i * per:(i + 1) * per]), d) for i, d in enumerate(ds)]
 
 
 def groups(cores, topo):
@@ -49,21 +59,31 @@ def plan(q, cores, topo):
     mine = first if q in first else rest
     urgent = [d for d in mine[::-1] if d != q and d in feeds]
     calm = [d for d in mine[::-1] if d > q and d not in feeds]
-    src, m = cores[q], None
-    for d in urgent + calm + ([feeds[q]] if q in feeds else []):
-        md = topo.mask(src, cores[d])
-        m = md if m is None else m & md
-    if m is None:
-        return [], 0
-    bits, calls = bits_of(m), []
-    if urgent:
-        per = 1
-        while per * 2 * len(urgent) <= len(bits):
-            per *= 2
-        calls.append([(sum(1 << b for b in bits[i * per:(i + 1) * per]), d) for i, d in enumerate(urgent)])
-    for d in calm:
-        calls.append([(trim(m), d)])
-    return calls, (trim(m) if q in feeds else 0)
+    src = cores[q]
+
+    def common(ds):
+        m = None
+        for d in ds:
+            md = topo.mask(src, cores[d])
+            m = md if m is None else m & md
+        return m or 0
+
+    on = common(urgent + calm)
+    off = common(rest) if q in first else 0
+    calls = []
+    if q in feeds:
+        spare = on & ~off
+        if calm and spare:
+            calls.append(split(on & off, urgent) + split(spare, calm))
+        else:
+            calls.append(split(on & off, urgent))
+            calls.extend([[(trim(on & off), d)] for d in calm])
+    else:
+        if urgent:
+            calls.append(split(on, urgent))
+        calls.extend([[(trim(on), d)] for d in calm])
+    straight = split(off, rest) if q in first else []
+    return calls, (trim(off) if q in feeds else 0), straight
 
 
 def rank_program(g, core, T, topo):
@@ -122,16 +142,22 @@ def rank_program(g, core, T, topo):
     def At(k):
         return T.pt[:, PT[k] * D:(PT[k] + 1) * D]
 
+    def cols(t, blk, lo, hi):
+        return t[:, blk * B + lo:blk * B + hi]
+
     def part(t, blk, h=None):
         if h is None:
-            return t[:, blk * B:(blk + 1) * B]
-        return t[:, blk * B + h * HW:blk * B + (h + 1) * HW]
+            return cols(t, blk, 0, B)
+        return cols(t, blk, h * HW, (h + 1) * HW)
 
     def X(s, h=None):
         return part(T.xs, s, h)
 
     def Lc(s, h=None):
         return X(0, h) if s == 0 else part(T.ls, s - 1, h)
+
+    def Lcols(s, lo, hi):
+        return cols(T.xs, 0, lo, hi) if s == 0 else cols(T.ls, s - 1, lo, hi)
 
     def Y(s, h=None):
         return part(T.ys, s, h)
@@ -140,37 +166,53 @@ def rank_program(g, core, T, topo):
         return part(T.land, q, h)
 
     LA, LT, LX0, LX1 = ("lda", 16), ("ldt", 16), ("ldx0", 16), ("ldx1", 16)
+    tA, tT = {1: LA}, {1: LT}
 
     g.sync.dma_start(A(1), T.a[:]).then_inc(sem.lda, 16)
     g.scalar.dma_start(T.xs[:, 0:2 * B], T.x[:, 0:2 * B]).then_inc(sem.ldx0, 16)
-    g.sync.dma_start(T.xs[:, 2 * B:4 * B], T.x[:, 2 * B:4 * B]).then_inc(sem.ldx1, 16)
-    if r > 0:
-        g.scalar.dma_start(At(1), T.at[:]).then_inc(sem.ldt, 16)
+    g.sync.dma_start(At(1), T.at[:]).then_inc(sem.ldt, 16)
+    g.scalar.dma_start(T.xs[:, 2 * B:4 * B], T.x[:, 2 * B:4 * B]).then_inc(sem.ldx1, 16)
 
-    tl = [[LX0, LX0]]
-    for s in range(1, S):
-        for h in range(2):
-            mm(2 * (s - 1) + h, 0, HW, A(1), Lc(s - 1, h), [LA, tl[s - 1][h]])
-        tl.append([vadd(Lc(s, h), 2 * (s - 1) + h, 0, HW, X(s, h), [LX0 if s < 2 else LX1]) for h in range(2)])
+    tl = {0: [LX0, LX0]}
+    for h in range(2):
+        mm(h, 0, HW, A(1), X(0, h), [LA, LX0])
+    b2 = nb()
+    mm(b2, 0, D, At(1), A(1), [LT, LA])
+    tl[1] = [vadd(Lc(1, h), h, 0, HW, X(1, h), [LX0]) for h in range(2)]
+    tA[2] = vcopy(A(2), b2, 0, D)
+    for h in range(2):
+        mm(2 + h, 0, HW, A(1), X(2, h), [LX1], start=True, stop=False)
+    for h in range(2):
+        mm(2 + h, 0, HW, A(2), Lc(1, h), [tA[2], tl[1][h]], start=False, stop=True)
+    tl[3] = [vadd(Lc(3, h), 2 + h, 0, HW, X(3, h), [LX1]) for h in range(2)]
+    for h in range(2):
+        mm(4 + h, 0, HW, A(1), Lc(1, h), [tl[1][h]])
+    tl[2] = [vadd(Lc(2, h), 4 + h, 0, HW, X(2, h), [LX1]) for h in range(2)]
 
-    calls, far_mask = plan(r, cores, topo)
-    sent = 0
-    if calls:
-        need("g", [tl[S - 1][1]])
-    for call in calls:
+    calls, far_mask, straight = plan(r, cores, topo)
+
+    def issue(call, src, dst, rsem):
         if len(call) == 1:
             mask, d = call[0]
             rid, pid = topo.addr(cores[d], core)
-            g.remote_dma(land(r), Lc(S - 1), sem["arr%d" % r], sem.sent, pid, rid, mask)
+            g.remote_dma(dst, src, rsem, sem.sent, pid, rid, mask)
         else:
             trs = []
             for mask, d in call:
                 rid, pid = topo.addr(cores[d], core)
                 trs.append(RemoteDMATransfer(dst_ids=[DstId(rid=rid, pnc=pid)], dma_engine_mask=mask,
-                                             remote_sem=sem["arr%d" % r], src=Lc(S - 1), dst=land(r)))
+                                             remote_sem=rsem, src=src, dst=dst))
             g.remote_dma_fused(trs, local_sem=sem.sent)
-        sent += sum(len(bits_of(mask)) for mask, d in call)
-    sent += 2 * len(bits_of(far_mask))
+        return sum(len(bits_of(mask)) for mask, d in call)
+
+    sent = 0
+    if calls:
+        need("g", [tl[S - 1][1]])
+    for i, call in enumerate(calls):
+        sent += issue(call, Lc(S - 1), land(r), sem["arr%d" % r])
+        if i == 0 and straight:
+            sent += issue(straight, Lcols(S - 1, 0, SW), T.sl[:, r * SW:(r + 1) * SW], sem.ars)
+    sent += len(CP) * len(bits_of(far_mask))
 
     def arrived(q):
         n = [len(bits_of(mask)) for call in plan(q, cores, topo)[0] for mask, d in call if d == r][0]
@@ -178,15 +220,16 @@ def rank_program(g, core, T, topo):
 
     stores = [0]
 
-    def store(s, n, deps):
+    def store_cols(lo, hi, deps):
         qn = "sy" if stores[0] % 2 == 0 else "sc"
         need(qn, deps)
-        queues[qn].dma_start(T.y[:, s * B:(s + n) * B], T.ys[:, s * B:(s + n) * B]).then_inc(sem.st, 16)
+        queues[qn].dma_start(T.y[:, lo:hi], T.ys[:, lo:hi]).then_inc(sem.st, 16)
         stores[0] += 1
 
-    pairs = r in feeds
+    def store(s, n, deps):
+        store_cols(s * B, (s + n) * B, deps)
 
-    tA, tT = {1: LA}, {1: LT}
+    pairs = r in feeds
 
     def emit_y(carry, tc):
         for s in range(S):
@@ -206,22 +249,22 @@ def rank_program(g, core, T, topo):
             elif s % 2 == 1:
                 store(s - 1, 2, [t])
 
-    def emit_far(koff, base, tbase, th):
-        for h in range(2):
+    def emit_far(koff, base, tbase, pieces):
+        for lo, hi, tok, slo in pieces:
             for s in range(S):
                 k = koff + s + 1
                 b = nb()
-                mm(b, 0, HW, A(k), part(T.hl, 0, h), [tA[k], th[h]])
-                t = vadd(Y(s, h), b, 0, HW, base(s, h), [tbase[s]])
-                if h == 1:
-                    store(s, 1, [t])
+                mm(b, 0, hi - lo, A(k), T.hl[:, lo:hi], [tA[k], tok])
+                t = vadd(cols(T.ys, s, lo, hi), b, 0, hi - lo, base(s, lo, hi), [tbase[s]])
+                if slo is not None:
+                    store_cols(s * B + slo, s * B + hi, [t])
 
     tls = [tl[s][1] for s in range(S)]
 
     if r == 0:
         need("sy", [LX0, ("sent", sent)])
         g.sync.dma_start(T.y[:, 0:B], X(0)).then_inc(sem.st, 16)
-        need("sc", [tl[S - 1][1], ("sent", sent)])
+        need("sc", [tl[2][1], ("sent", sent)])
         g.scalar.dma_start(T.y[:, B:S * B], T.ls[:]).then_inc(sem.st, 16)
         stores[0] = 2
     else:
@@ -230,22 +273,17 @@ def rank_program(g, core, T, topo):
             mm(b, 0, n * D, lhsT, rhs, deps)
             return vcopy(out, b, 0, n * D)
 
-        tA[2] = power(A(2), At(1), A(1), 1, [LT, LA])
-        tT[2] = power(At(2), A(1), At(1), 1, [])
+        tT[2] = power(At(2), A(1), At(1), 1, [LT, LA])
         if r in feeds:
-            def Lq(q, h):
-                return Lc(S - 1, h) if q == r else land(q, h)
+            def Lq(q, lo, hi):
+                return Lcols(S - 1, lo, hi) if q == r else cols(T.land, q, lo, hi)
 
-            def tq(q, h):
-                return tl[S - 1][h] if q == r else arrived(q)
+            def tq(q):
+                return tl[S - 1][1] if q == r else arrived(q)
 
             qs = sorted(range(K - 1), key=lambda q: (q != r, q not in feeds, -q))
-            hb = [nb(), nb()]
+            hb = [nb() for p in CP]
             kept.extend(hb)
-
-            def term(q, h):
-                k = 4 * (K - 1 - q)
-                mm(hb[h], 0, HW, A(k), Lq(q, h), [tA[k], tq(q, h)], start=(q == qs[0]), stop=(q == qs[-1]))
 
             tA[4] = power(A(4), At(2), A(2), 1, [tA[2], tT[2]])
             tT[4] = power(At(4), A(2), At(2), 1, [])
@@ -253,21 +291,25 @@ def rank_program(g, core, T, topo):
             tA[8] = power(A(8), At(4), A(4), 1, [tA[4], tT[4]])
             tA[12] = power(A(12), At(4), A(8), 1, [tA[8]])
             for q in qs:
-                for h in range(2):
-                    term(q, h)
-            th = [vadd(part(T.hs, 0, h), hb[h], 0, HW, land(K - 1, h), [arrived(K - 1)]) for h in range(2)]
+                k = 4 * (K - 1 - q)
+                for p, (lo, hi) in enumerate(CP):
+                    mm(hb[p], 0, hi - lo, A(k), Lq(q, lo, hi), [tA[k], tq(q)], start=(q == qs[0]), stop=(q == qs[-1]))
+            th = [vadd(T.hs[:, lo:hi], hb[p], 0, hi - lo, cols(T.land, K - 1, lo, hi), [arrived(K - 1)])
+                  for p, (lo, hi) in enumerate(CP)]
             kept.clear()
             rid, pid = topo.addr(cores[feeds[r]], core)
-            for h in range(2):
-                need("g", [th[h]])
-                g.remote_dma(part(T.hl, 0, h), part(T.hs, 0, h), sem["arrh%d" % h], sem.sent, pid, rid, far_mask)
+            for p, (lo, hi) in enumerate(CP):
+                need("g", [th[p]])
+                g.remote_dma(T.hl[:, lo:hi], T.hs[:, lo:hi], sem["arrh%d" % p], sem.sent, pid, rid, far_mask)
         else:
             tA[3] = tA[4] = power(A(3, 2), At(2), A(1, 2), 2, [tA[2], tT[2]])
             tT[4] = power(At(4), A(2), At(2), 1, [])
             if r in rest[1:]:
                 tA[5] = tA[6] = tA[7] = tA[8] = power(A(5, 4), At(4), A(1, 4), 4, [tA[4], tT[4]])
-            elif r in first:
+            else:
                 tA[8] = power(A(8), At(4), A(4), 1, [tA[4], tT[4]])
+            if r in rest:
+                tA[12] = power(A(12), At(4), A(8), 1, [tA[8]])
 
         if r in first:
             if r == 1:
@@ -284,16 +326,26 @@ def rank_program(g, core, T, topo):
         else:
             src_rank = [f for f in feeds if feeds[f] == r][0]
             n = len(bits_of(plan(src_rank, cores, topo)[1]))
-            th = [("arrh0", n), ("arrh1", n)]
+            ARS = ("ars", sum(len(bits_of(mask)) for q in first for mask, d in plan(q, cores, topo)[2] if d == r))
             if r == rest[0]:
-                emit_far(0, Lc, tls, th)
+                koff, base, tbase = 0, Lcols, tls
             else:
-                tb = []
+                tbase = []
                 for s in range(S):
                     b = nb()
                     mm(b, 0, B, A(s + 1), land(r - 1), [tA[s + 1], arrived(r - 1)])
-                    tb.append(vadd(part(T.bs, s), b, 0, B, Lc(s), [tls[s]]))
-                emit_far(S, lambda s, h: part(T.bs, s, h), tb, th)
+                    tbase.append(vadd(part(T.bs, s), b, 0, B, Lc(s), [tls[s]]))
+                koff, base = S, (lambda s, lo, hi: cols(T.bs, s, lo, hi))
+            sb = nb()
+            kept.append(sb)
+            for q in range(K - 1):
+                k = 4 * (K - 1 - q)
+                mm(sb, 0, SW, A(k), T.sl[:, q * SW:(q + 1) * SW], [tA[k], ARS], start=(q == 0), stop=(q == K - 2))
+            ts = vadd(T.hl[:, 0:SW], sb, 0, SW, T.sl[:, (K - 1) * SW:K * SW], [ARS])
+            kept.clear()
+            emit_far(koff, base, tbase, [(0, SW, ts, None),
+                                         (CP[0][0], CP[0][1], ("arrh0", n), 0),
+                                         (CP[1][0], CP[1][1], ("arrh1", n), CP[1][0])])
 
     if sent:
         g.wait_ge(sem.sent, sent)

from concourse.bass import DstId, RemoteDMATransfer
from concourse.mybir import AluOpType

N, S, B, D = 6, 4, 256, 128
HW = B // 2
SW = 64
CP = [(SW, SW + (B - SW) // 2), (SW + (B - SW) // 2, B)]
PW = {1: 0, 2: 1, 3: 2, 4: 3, 5: 4, 6: 5, 7: 6, 8: 7, 12: 8}
PT = {1: 0, 2: 1, 4: 2}

SCRATCH = {
    "xs": ("sbuf", [128, S * B], "bfloat16"),
    "pw": ("sbuf", [128, len(PW) * D], "bfloat16"),
    "pt": ("sbuf", [128, len(PT) * D], "bfloat16"),
    "ls": ("sbuf", [128, (S - 1) * B], "bfloat16"),
    "land": ("sbuf", [128, (N - 1) * B], "bfloat16"),
    "sl": ("sbuf", [128, N * SW], "bfloat16"),
    "hs": ("sbuf", [128, B], "bfloat16"),
    "hl": ("sbuf", [128, B], "bfloat16"),
    "cb": ("sbuf", [128, B], "bfloat16"),
    "bs": ("sbuf", [128, S * B], "bfloat16"),
    "ys": ("sbuf", [128, S * B], "bfloat16"),
}
for i in range(8):
    SCRATCH["b%d" % i] = ("psum", [128, 512], "float32")

SEMAPHORES = (["lda", "ldt", "ldx0", "ldx1", "pe", "ve", "sent", "st", "arrh0", "arrh1", "ars"]
              + ["arr%d" % q for q in range(N - 1)])


def bits_of(m):
    return [b for b in range(m.bit_length()) if (m >> b) & 1]


def trim(m):
    bits, n = bits_of(m), 1
    while n * 2 <= len(bits):
        n *= 2
    return sum(1 << b for b in bits[:n])


def split(m, ds):
    bits, per = bits_of(m), 1
    while per * 2 * len(ds) <= len(bits):
        per *= 2
    return [(sum(1 << b for b in bits[i * per:(i + 1) * per]), d) for i, d in enumerate(ds)]


def groups(cores, topo):
    place = [(topo.host(c), topo.chip(c)) for c in cores]
    first = [i for i in range(len(cores)) if place[i] == place[0]]
    rest = [i for i in range(len(cores)) if place[i] != place[0]]
    feeds = {first[-2 - j]: d for j, d in enumerate(rest)}
    return first, rest, feeds


def plan(q, cores, topo):
    first, rest, feeds = groups(cores, topo)
    mine = first if q in first else rest
    urgent = [d for d in mine[::-1] if d != q and d in feeds]
    calm = [d for d in mine[::-1] if d > q and d not in feeds]
    src = cores[q]

    def common(ds):
        m = None
        for d in ds:
            md = topo.mask(src, cores[d])
            m = md if m is None else m & md
        return m or 0

    on = common(urgent + calm)
    off = common(rest) if q in first else 0
    calls = []
    if q in feeds:
        spare = on & ~off
        if calm and spare:
            calls.append(split(on & off, urgent) + split(spare, calm))
        else:
            calls.append(split(on & off, urgent))
            calls.extend([[(trim(on & off), d)] for d in calm])
    else:
        if urgent:
            calls.append(split(on, urgent))
        calls.extend([[(trim(on), d)] for d in calm])
    straight = split(off, rest) if q in first else []
    return calls, (trim(off) if q in feeds else 0), straight


def rank_program(g, core, T, topo):
    r = T.rank_of(core)
    if r is None:
        return
    cores = list(T.cores)
    sem = T.sem
    first, rest, feeds = groups(cores, topo)
    K = len(first)
    queues = {"pe": g.tensor, "ve": g.vector, "sy": g.sync, "sc": g.scalar, "g": g}
    done = {"pe": 0, "ve": 0}
    seen = {}
    bank = [T["b%d" % k] for k in range(8)]
    last_on = {}
    nxt = [6]
    kept = []

    def nb():
        b = nxt[0]
        while b in kept:
            b = (b + 1) % 8
        nxt[0] = (b + 1) % 8
        return b

    def need(qn, toks):
        for name, val in toks:
            if seen.get((qn, name), 0) < val:
                queues[qn].wait_ge(sem[name], val)
                seen[(qn, name)] = val

    def mm(b, lo, hi, lhsT, rhs, deps, start=True, stop=True):
        need("pe", list(deps) + last_on.get((b, "ve"), []))
        g.tensor.matmul(bank[b][:, lo:hi], lhsT, rhs, start, stop).then_inc(sem.pe, 1)
        done["pe"] += 1
        last_on[(b, "pe")] = [("pe", done["pe"])]
        return ("pe", done["pe"])

    def vadd(out, b, lo, hi, in1, deps):
        need("ve", list(deps) + last_on[(b, "pe")])
        g.vector.tensor_tensor(out, bank[b][:, lo:hi], in1, AluOpType.add).then_inc(sem.ve, 1)
        done["ve"] += 1
        last_on[(b, "ve")] = [("ve", done["ve"])]
        return ("ve", done["ve"])

    def vcopy(out, b, lo, hi):
        need("ve", last_on[(b, "pe")])
        g.vector.tensor_copy(out, bank[b][:, lo:hi]).then_inc(sem.ve, 1)
        done["ve"] += 1
        last_on[(b, "ve")] = [("ve", done["ve"])]
        return ("ve", done["ve"])

    def A(k, n=1):
        return T.pw[:, PW[k] * D:(PW[k] + n) * D]

    def At(k):
        return T.pt[:, PT[k] * D:(PT[k] + 1) * D]

    def cols(t, blk, lo, hi):
        return t[:, blk * B + lo:blk * B + hi]

    def part(t, blk, h=None):
        if h is None:
            return cols(t, blk, 0, B)
        return cols(t, blk, h * HW, (h + 1) * HW)

    def X(s, h=None):
        return part(T.xs, s, h)

    def Lc(s, h=None):
        return X(0, h) if s == 0 else part(T.ls, s - 1, h)

    def Lcols(s, lo, hi):
        return cols(T.xs, 0, lo, hi) if s == 0 else cols(T.ls, s - 1, lo, hi)

    def Y(s, h=None):
        return part(T.ys, s, h)

    def land(q, h=None):
        return part(T.land, q, h)

    LA, LT, LX0, LX1 = ("lda", 16), ("ldt", 16), ("ldx0", 16), ("ldx1", 16)
    tA, tT = {1: LA}, {1: LT}

    g.sync.dma_start(A(1), T.a[:]).then_inc(sem.lda, 16)
    g.scalar.dma_start(T.xs[:, 0:2 * B], T.x[:, 0:2 * B]).then_inc(sem.ldx0, 16)
    g.sync.dma_start(At(1), T.at[:]).then_inc(sem.ldt, 16)
    g.scalar.dma_start(T.xs[:, 2 * B:4 * B], T.x[:, 2 * B:4 * B]).then_inc(sem.ldx1, 16)

    tl = {0: [LX0, LX0]}
    for h in range(2):
        mm(h, 0, HW, A(1), X(0, h), [LA, LX0])
    b2 = nb()
    mm(b2, 0, D, At(1), A(1), [LT, LA])
    tl[1] = [vadd(Lc(1, h), h, 0, HW, X(1, h), [LX0]) for h in range(2)]
    tA[2] = vcopy(A(2), b2, 0, D)
    for h in range(2):
        mm(2 + h, 0, HW, A(1), X(2, h), [LX1], start=True, stop=False)
    for h in range(2):
        mm(2 + h, 0, HW, A(2), Lc(1, h), [tA[2], tl[1][h]], start=False, stop=True)
    tl[3] = [vadd(Lc(3, h), 2 + h, 0, HW, X(3, h), [LX1]) for h in range(2)]
    for h in range(2):
        mm(4 + h, 0, HW, A(1), Lc(1, h), [tl[1][h]])
    tl[2] = [vadd(Lc(2, h), 4 + h, 0, HW, X(2, h), [LX1]) for h in range(2)]

    calls, far_mask, straight = plan(r, cores, topo)

    def issue(call, src, dst, rsem):
        if len(call) == 1:
            mask, d = call[0]
            rid, pid = topo.addr(cores[d], core)
            g.remote_dma(dst, src, rsem, sem.sent, pid, rid, mask)
        else:
            trs = []
            for mask, d in call:
                rid, pid = topo.addr(cores[d], core)
                trs.append(RemoteDMATransfer(dst_ids=[DstId(rid=rid, pnc=pid)], dma_engine_mask=mask,
                                             remote_sem=rsem, src=src, dst=dst))
            g.remote_dma_fused(trs, local_sem=sem.sent)
        return sum(len(bits_of(mask)) for mask, d in call)

    sent = 0
    if calls:
        need("g", [tl[S - 1][1]])
    for i, call in enumerate(calls):
        sent += issue(call, Lc(S - 1), land(r), sem["arr%d" % r])
        if i == 0 and straight:
            sent += issue(straight, Lcols(S - 1, 0, SW), T.sl[:, r * SW:(r + 1) * SW], sem.ars)
    sent += len(CP) * len(bits_of(far_mask))

    def arrived(q):
        n = [len(bits_of(mask)) for call in plan(q, cores, topo)[0] for mask, d in call if d == r][0]
        return ("arr%d" % q, n)

    stores = [0]

    def store_cols(lo, hi, deps):
        qn = "sy" if stores[0] % 2 == 0 else "sc"
        need(qn, deps)
        queues[qn].dma_start(T.y[:, lo:hi], T.ys[:, lo:hi]).then_inc(sem.st, 16)
        stores[0] += 1

    def store(s, n, deps):
        store_cols(s * B, (s + n) * B, deps)

    pairs = r in feeds

    def emit_y(carry, tc):
        for s in range(S):
            k = s + 1
            if s in (0, S - 1):
                bb = [nb(), nb()]
                for h in range(2):
                    mm(bb[h], 0, HW, A(k), carry(h), [tA[k], tc[h]])
                for h in range(2):
                    t = vadd(Y(s, h), bb[h], 0, HW, Lc(s, h), [tls[s]])
            else:
                b = nb()
                mm(b, 0, B, A(k), carry(None), [tA[k], tc[0], tc[1]])
                t = vadd(Y(s), b, 0, B, Lc(s), [tls[s]])
            if not pairs:
                store(s, 1, [t])
            elif s % 2 == 1:
                store(s - 1, 2, [t])

    def emit_far(koff, base, tbase, pieces):
        for lo, hi, tok, slo in pieces:
            for s in range(S):
                k = koff + s + 1
                b = nb()
                mm(b, 0, hi - lo, A(k), T.hl[:, lo:hi], [tA[k], tok])
                t = vadd(cols(T.ys, s, lo, hi), b, 0, hi - lo, base(s, lo, hi), [tbase[s]])
                if slo is not None:
                    store_cols(s * B + slo, s * B + hi, [t])

    tls = [tl[s][1] for s in range(S)]

    if r == 0:
        need("sy", [LX0, ("sent", sent)])
        g.sync.dma_start(T.y[:, 0:B], X(0)).then_inc(sem.st, 16)
        need("sc", [tl[2][1], ("sent", sent)])
        g.scalar.dma_start(T.y[:, B:S * B], T.ls[:]).then_inc(sem.st, 16)
        stores[0] = 2
    else:
        def power(out, lhsT, rhs, n, deps):
            b = nb()
            mm(b, 0, n * D, lhsT, rhs, deps)
            return vcopy(out, b, 0, n * D)

        tT[2] = power(At(2), A(1), At(1), 1, [LT, LA])
        if r in feeds:
            def Lq(q, lo, hi):
                return Lcols(S - 1, lo, hi) if q == r else cols(T.land, q, lo, hi)

            def tq(q):
                return tl[S - 1][1] if q == r else arrived(q)

            qs = sorted(range(K - 1), key=lambda q: (q != r, q not in feeds, -q))
            hb = [nb() for p in CP]
            kept.extend(hb)

            tA[4] = power(A(4), At(2), A(2), 1, [tA[2], tT[2]])
            tT[4] = power(At(4), A(2), At(2), 1, [])
            tA[3] = power(A(3), At(2), A(1), 1, [])
            tA[8] = power(A(8), At(4), A(4), 1, [tA[4], tT[4]])
            tA[12] = power(A(12), At(4), A(8), 1, [tA[8]])
            for q in qs:
                k = 4 * (K - 1 - q)
                for p, (lo, hi) in enumerate(CP):
                    mm(hb[p], 0, hi - lo, A(k), Lq(q, lo, hi), [tA[k], tq(q)], start=(q == qs[0]), stop=(q == qs[-1]))
            th = [vadd(T.hs[:, lo:hi], hb[p], 0, hi - lo, cols(T.land, K - 1, lo, hi), [arrived(K - 1)])
                  for p, (lo, hi) in enumerate(CP)]
            kept.clear()
            rid, pid = topo.addr(cores[feeds[r]], core)
            for p, (lo, hi) in enumerate(CP):
                need("g", [th[p]])
                g.remote_dma(T.hl[:, lo:hi], T.hs[:, lo:hi], sem["arrh%d" % p], sem.sent, pid, rid, far_mask)
        else:
            tA[3] = tA[4] = power(A(3, 2), At(2), A(1, 2), 2, [tA[2], tT[2]])
            tT[4] = power(At(4), A(2), At(2), 1, [])
            if r in rest[1:]:
                tA[5] = tA[6] = tA[7] = tA[8] = power(A(5, 4), At(4), A(1, 4), 4, [tA[4], tT[4]])
            else:
                tA[8] = power(A(8), At(4), A(4), 1, [tA[4], tT[4]])
            if r in rest:
                tA[12] = power(A(12), At(4), A(8), 1, [tA[8]])

        if r in first:
            if r == 1:
                emit_y(lambda h: land(0, h), [arrived(0), arrived(0)])
            else:
                cbk = [nb(), nb()]
                qs = list(range(r - 1))
                for q in qs:
                    for h in range(2):
                        k = 4 * (r - 1 - q)
                        mm(cbk[h], 0, HW, A(k), land(q, h), [tA[k], arrived(q)], start=(q == qs[0]), stop=(q == qs[-1]))
                tc = [vadd(part(T.cb, 0, h), cbk[h], 0, HW, land(r - 1, h), [arrived(r - 1)]) for h in range(2)]
                emit_y(lambda h: part(T.cb, 0, h), tc)
        else:
            src_rank = [f for f in feeds if feeds[f] == r][0]
            n = len(bits_of(plan(src_rank, cores, topo)[1]))
            ARS = ("ars", sum(len(bits_of(mask)) for q in first for mask, d in plan(q, cores, topo)[2] if d == r))
            if r == rest[0]:
                koff, base, tbase = 0, Lcols, tls
            else:
                tbase = []
                for s in range(S):
                    b = nb()
                    mm(b, 0, B, A(s + 1), land(r - 1), [tA[s + 1], arrived(r - 1)])
                    tbase.append(vadd(part(T.bs, s), b, 0, B, Lc(s), [tls[s]]))
                koff, base = S, (lambda s, lo, hi: cols(T.bs, s, lo, hi))
            sb = nb()
            kept.append(sb)
            for q in range(K - 1):
                k = 4 * (K - 1 - q)
                mm(sb, 0, SW, A(k), T.sl[:, q * SW:(q + 1) * SW], [tA[k], ARS], start=(q == 0), stop=(q == K - 2))
            ts = vadd(T.hl[:, 0:SW], sb, 0, SW, T.sl[:, (K - 1) * SW:K * SW], [ARS])
            kept.clear()
            emit_far(koff, base, tbase, [(0, SW, ts, None),
                                         (CP[0][0], CP[0][1], ("arrh0", n), 0),
                                         (CP[1][0], CP[1][1], ("arrh1", n), CP[1][0])])

    if sent:
        g.wait_ge(sem.sent, sent)
    g.wait_ge(sem.st, 16 * stores[0])
